import numpy as np
import ml_dtypes


def mxq(x, axis, fmt="e4m3"):
    dtype, down = {"e4m3": (ml_dtypes.float8_e4m3fn, 7), "e5m2": (ml_dtypes.float8_e5m2, 14)}[fmt]
    v = np.moveaxis(np.asarray(x, np.float32).astype(ml_dtypes.bfloat16).astype(np.float64), axis, -1)
    blocks = v.reshape(v.shape[:-1] + (-1, 32))
    amax = np.abs(blocks).max(-1, keepdims=True)
    byte = np.maximum(np.where(amax > 0, np.frexp(amax)[1] - 1 + 127, 0) - down, 1)
    scale = np.exp2(byte - 127.0)
    codes = (blocks / scale).astype(np.float32).astype(dtype).astype(np.float64)
    return np.moveaxis((codes * scale).reshape(v.shape), -1, axis)


WIDE = False


def mx_kscale(k):
    if not WIDE:
        return np.ones(k)
    levels = np.array([10, -10, 5, -5, 0])
    if k % 512:
        return np.exp2(np.random.permutation(np.resize(levels, k // 32))).repeat(32)
    a = np.empty((k // 512, 16))
    for p in range(k // 512):
        a[p, :8] = np.random.permutation(np.resize(levels, 8))
        for g in range(8):
            far = levels[np.abs(levels - a[p, g]) >= 10]
            a[p, g + 8] = far[np.random.randint(len(far))]
    return np.exp2(a.ravel()).repeat(32)


def f64(x):
    return np.asarray(x).astype(np.float64)


def striped(idx):
    return np.tile(idx.reshape(-1, 16).T, (8, 1)).astype(np.uint16)


def unstriped(offs):
    return offs[:16].T.reshape(-1).astype(np.int64)


E2M1 = np.array([0.0, 0.5, 1.0, 1.5, 2.0, 3.0, 4.0, 6.0, -0.0, -0.5, -1.0, -1.5, -2.0, -3.0, -4.0, -6.0])


def pack_weight(w, fmt):
    k, n = w.shape
    w = f64(np.asarray(w, np.float32).astype(ml_dtypes.bfloat16)).reshape(k // 32, 32, n)
    amax = np.abs(w).max(1)
    if fmt == "e4m3":
        byte = np.frexp(amax)[1] - 1 + 127 - 7
    else:
        mant, ex = np.frexp(amax / 6.0)
        byte = np.where(mant > 0.5, ex, ex - 1) + 127
    byte = np.clip(np.where(amax > 0, byte, 1), 1, 254)
    scaled = (w * np.exp2(127.0 - byte)[:, None, :]).reshape(k, n).astype(np.float32)
    by_word = np.ascontiguousarray(scaled.reshape(k // 512, 128, 4, n).transpose(0, 1, 3, 2))
    if fmt == "e4m3":
        words = by_word.astype(ml_dtypes.float8_e4m3fn).view(np.uint8)
    else:
        c = by_word.astype(ml_dtypes.float4_e2m1fn).view(np.uint8) & 0xF
        words = (c[..., 0::2] | (c[..., 1::2] << 4)).reshape(k // 512, 128, 2 * n)
    return np.ascontiguousarray(words), np.ascontiguousarray(byte.astype(np.uint8).reshape(k // 512, 16, n))


def unpack_weight(words, scales, fmt):
    g, _, n = scales.shape
    words = np.ascontiguousarray(words).reshape(g, 128, n, -1)
    if fmt == "e4m3":
        vals = words.view(ml_dtypes.float8_e4m3fn).astype(np.float64)
    else:
        nib = np.empty((g, 128, n, 4), np.uint8)
        nib[..., 0::2] = words & 0xF
        nib[..., 1::2] = words >> 4
        vals = E2M1[nib]
    vals = vals * np.repeat(np.exp2(scales.astype(np.float64) - 127.0), 8, axis=1)[..., None]
    return vals.transpose(0, 1, 3, 2).reshape(g * 512, n)


def gelu(v):
    return 0.5 * v * (1.0 + np.tanh(np.sqrt(2.0 / np.pi) * (v + 0.044715 * v**3)))


def bf(x):
    return np.asarray(x, np.float32).astype(ml_dtypes.bfloat16)


def planes(Y):
    n, m = Y.shape
    b = f64(bf(Y)).reshape(n // 32, 32, m)
    amax = np.abs(b).max(1)
    byte = np.clip(np.where(amax > 0, np.frexp(amax)[1] - 1 + 127 - 7, 1), 1, 254)
    codes = (b * np.exp2(127.0 - byte)[:, None, :]).reshape(n, m).astype(np.float32).astype(ml_dtypes.float8_e4m3fn).view(np.uint8)
    words = codes.reshape(n // 512, 128, 4, m).transpose(0, 1, 3, 2)
    return np.ascontiguousarray(words), np.ascontiguousarray(byte.astype(np.uint8).reshape(n // 512, 16, m))


T, S, K, K2, M, H, N, T2 = 2048, 512, 1024, 512, 512, 1024, 512, 1024

def setup_inputs():
    n = np.random.standard_normal
    s1, s2 = mx_kscale(K)[:, None], mx_kscale(K2)[:, None]
    um, u = mx_kscale(M)[:, None], mx_kscale(H)[:, None]
    size = np.exp(0.8 * n(N))
    tab_words, tab_scales = pack_weight(n((K, T)) * s1, "e4m3")
    tab2_words, tab2_scales = pack_weight(n((K2, T)) * s2, "e4m3")
    w2_words, w2_scales = pack_weight(n((K2, M)) * (1.5 / np.sqrt(K2)) / s2, "e2m1")
    w4_words, w4_scales = pack_weight(n((H, N)) / np.sqrt(H) / u * size[None, :], "e2m1")
    return {
        "tab_words": tab_words, "tab_scales": tab_scales,
        "tab2_words": tab2_words, "tab2_scales": tab2_scales,
        "offs": striped(np.random.permutation(T)[:S]),
        "offs2": striped(np.random.permutation(T)[:S]),
        "offs3": striped(np.random.permutation(T2)[:S]),
        "offs4": striped(np.random.permutation(T2)[:S]),
        "w1": (n((K, H)) * (1.5 / np.sqrt(K)) / s1).astype(np.float32),
        "g1": (1.3 * np.exp(0.3 * n(H)) * u[:, 0]).astype(np.float32),
        "w2_words": w2_words, "w2_scales": w2_scales,
        "g2": (np.exp(0.3 * n(M)) * um[:, 0]).astype(np.float32),
        "w3": (n((M, H)) / np.sqrt(M) / um * u.T).astype(np.float32),
        "wg1": np.exp(0.3 * n((128, S))).astype(np.float32),
        "wg2": np.exp(0.3 * n((128, S))).astype(np.float32),
        "cat": (0.7 * n((H, T2)) * u).astype(np.float32),
        "w4_words": w4_words, "w4_scales": w4_scales,
        "res": (0.6 * n((N, T2)) * size[:, None]).astype(np.float32),
    }

def reference(tab_words, tab_scales, tab2_words, tab2_scales, offs, offs2, offs3, offs4, w1, g1, w2_words, w2_scales, g2, w3, wg1, wg2, cat, w4_words, w4_scales, res):
    v = unpack_weight(tab_words, tab_scales, "e4m3")[:, unstriped(offs)]
    v2 = unpack_weight(tab2_words, tab2_scales, "e4m3")[:, unstriped(offs2)]
    h1 = np.tanh(mxq(f64(w1), 0, "e4m3").T @ v) * f64(g1)[:, None]
    b = unpack_weight(w2_words, w2_scales, "e2m1").T @ v2
    d = b / (1.0 + np.exp(-b)) * f64(g2)[:, None]
    h2 = mxq(f64(w3), 0, "e4m3").T @ mxq(d, 0, "e4m3")
    pa = np.zeros((H, T2))
    pa[:, unstriped(offs3)] = np.tile(f64(wg1), (H // 128, 1)) * h1
    pb = np.zeros((H, T2))
    pb[:, unstriped(offs4)] = np.tile(f64(wg2), (H // 128, 1)) * h2
    z = np.maximum(pa + f64(cat), pb)
    y = (unpack_weight(w4_words, w4_scales, "e2m1").T @ mxq(z, 0, "e4m3")) + f64(res)
    words, scales = planes(y)
    return y, words, scales

@@ -1,0 +1,319 @@
+from contextlib import ExitStack
+
+import concourse.mybir as mybir
+from concourse.masks import make_identity
+
+F32 = mybir.dt.float32
+BF16 = mybir.dt.bfloat16
+I32 = mybir.dt.int32
+U32 = mybir.dt.uint32
+U16 = mybir.dt.uint16
+U8 = mybir.dt.uint8
+FP8X4 = mybir.dt.float8_e4m3fn_x4
+FP4X4 = mybir.dt.float4_e2m1fn_x4
+ACT = mybir.ActivationFunctionType
+ALU = mybir.AluOpType
+
+T, S, K, K2, M, H, N, T2 = 2048, 512, 1024, 512, 512, 1024, 512, 1024
+FLOPS = 2 * S * (K * H + K2 * M + M * H) + 2 * H * N * T2
+
+P = 128
+PACK = 4
+BANK = 512
+SLICES = H // P
+W_CHUNK = 256
+Y_CHUNK = 256
+
+
+def tile_list_transit_vetting_pages_kernel(
+    tc, tab_words, tab_scales, tab2_words, tab2_scales, offs, offs2, offs3, offs4,
+    w1, g1, w2_words, w2_scales, g2, w3, wg1, wg2, cat, w4_words, w4_scales, res,
+    out_0, out_1, out_2,
+):
+    nc = tc.nc
+    with ExitStack() as ctx:
+        sb = ctx.enter_context(tc.tile_pool(name="sb", bufs=1))
+        ps = ctx.enter_context(tc.psum_pool(name="ps", bufs=1))
+
+        def held(name, shape, dtype):
+            return sb.tile(shape, dtype, name=name, align_bytes=64)
+
+        def shared(tag, bufs, name, shape, dtype):
+            return sb.tile(shape, dtype, name=name, tag=tag, bufs=bufs, align_bytes=64)
+
+        banks = [ps.tile([P, BANK], F32, name="bank%d" % b) for b in range(8)]
+
+        list_v = held("list_v", [P, S // 16], U16)
+        list_v2 = held("list_v2", [P, S // 16], U16)
+        list_pa = held("list_pa", [P, S // 16], U16)
+        list_pb = held("list_pb", [P, S // 16], U16)
+
+        v_words = [shared("table", 3, "v_words%d" % a, [P, T], U32) for a in range(2)]
+        v_scales = held("v_scales", [P, T], U8)
+        v2_words = shared("table", 3, "v2_words", [P, T], U32)
+        v2_scales = held("v2_scales", [P, T], U8)
+        w2_raw = held("w2_raw", [P, 2 * M], U8)
+        w2_raw_scales = held("w2_raw_scales", [P, M], U8)
+        w4_raw = held("w4_raw", [P, 2, 2 * N], U8)
+        w4_raw_scales = held("w4_raw_scales", [P, 2, N], U8)
+        pages_a = [held("page_a%d" % i, [P, T2], F32) for i in range(2)]
+        pages_b = [held("page_b%d" % i, [P, T2], F32) for i in range(2)]
+
+        for plane in (v2_scales, w2_raw_scales, v_scales):
+            nc.vector.memset(plane[:].bitcast(I32), 0)
+        nc.vector.memset(w4_raw_scales[:].rearrange("p a n -> p (a n)").bitcast(I32), 0)
+        ident = held("ident", [P, P], F32)
+        make_identity(nc, ident[:])
+        for page in (pages_a[0], pages_b[0], pages_a[1], pages_b[1]):
+            nc.gpsimd.memset(page[:], 0.0)
+
+        g1_cols = held("g1_cols", [P, SLICES], F32)
+        g2_cols = held("g2_cols", [P, PACK], F32)
+        wg1_sb = held("wg1_sb", [P, S], F32)
+        wg2_sb = held("wg2_sb", [P, S], F32)
+        n_chunks = H // W_CHUNK
+        w_raw = [[shared("stage", 12, "w_raw%d_%d" % (i, a), [P, PACK, W_CHUNK], F32) for a in range(3)] for i in range(n_chunks)]
+        cat_sb = [held("cat%d" % c, [P, T2], F32) for c in range(SLICES)]
+
+        def words_of(dram):
+            return dram.rearrange("p t i -> p (t i)").bitcast(I32)
+
+        def load_weights(i):
+            cols = slice(i * W_CHUNK, (i + 1) * W_CHUNK)
+            for a, rows in enumerate((w1[0:512, :], w1[512:1024, :], w3)):
+                nc.sync.dma_start(out=w_raw[i][a][:], in_=rows.rearrange("(p j) w -> p j w", j=PACK)[:, :, cols])
+
+        def load_cat(c):
+            nc.sync.dma_start(out=cat_sb[c][:], in_=cat[c * P:(c + 1) * P, :])
+
+        nc.sync.dma_start(out=v2_words[:].bitcast(I32), in_=words_of(tab2_words[0]))
+        for q in range(4):
+            nc.sync.dma_start(out=v2_scales[32 * q:32 * q + 4, :].bitcast(I32), in_=tab2_scales[0, 4 * q:4 * q + 4, :].bitcast(I32))
+        nc.sync.dma_start(list_v2[:], offs2)
+        nc.sync.dma_start(out=w2_raw[:].bitcast(I32), in_=w2_words[0].bitcast(I32))
+        nc.sync.dma_start(out=v_words[0][:].bitcast(I32), in_=words_of(tab_words[0]))
+        for q in range(4):
+            nc.sync.dma_start(out=w2_raw_scales[32 * q:32 * q + 4, :].bitcast(I32), in_=w2_scales[0, 4 * q:4 * q + 4, :].bitcast(I32))
+        nc.sync.dma_start(list_v[:], offs)
+        nc.sync.dma_start(out=g2_cols[:], in_=g2.rearrange("(p t) -> p t", t=PACK))
+        nc.sync.dma_start(out=v_words[1][:].bitcast(I32), in_=words_of(tab_words[1]))
+        for q in range(4):
+            nc.sync.dma_start(out=v_scales[32 * q:32 * q + 8, :].bitcast(I32), in_=tab_scales[:, 4 * q:4 * q + 4, :].bitcast(I32))
+        load_weights(0)
+        with nc.allow_non_contiguous_dma(reason="one gain for each partition and slice"):
+            nc.sync.dma_start(out=g1_cols[:], in_=g1.rearrange("(c p) -> p c", p=P))
+        nc.sync.dma_start(out=wg1_sb[:], in_=wg1)
+        nc.sync.dma_start(list_pa[:], offs3)
+        nc.sync.dma_start(out=wg2_sb[:], in_=wg2)
+        nc.sync.dma_start(list_pb[:], offs4)
+        for i in range(1, n_chunks):
+            load_cat(i - 1)
+            load_weights(i)
+        load_cat(n_chunks - 1)
+        nc.sync.dma_start(out=w4_raw[:].bitcast(I32), in_=w4_words.rearrange("a p n -> p a n").bitcast(I32))
+        for q in range(4):
+            nc.sync.dma_start(
+                out=w4_raw_scales[32 * q:32 * q + 4, :, :].bitcast(I32),
+                in_=w4_scales[:, 4 * q:4 * q + 4, :].rearrange("a r n -> r a n").bitcast(I32),
+            )
+        for c in range(n_chunks, SLICES):
+            load_cat(c)
+
+        w2_dealt = held("w2_dealt", [P, PACK, 2 * P], U8)
+        w2_dealt_scales = held("w2_dealt_scales", [P, PACK, P], U8)
+        nc.vector.tensor_copy(
+            out=w2_dealt[:].rearrange("p t (q b) -> p t q b", b=2),
+            in_=w2_raw[:].rearrange("p (q t b) -> p t q b", t=PACK, b=2),
+        )
+        nc.vector.tensor_copy(out=w2_dealt_scales[:], in_=w2_raw_scales[:].rearrange("p (q t) -> p t q", t=PACK))
+
+        v2_picked = held("v2_picked", [P, S], U32)
+        v2_picked_scales = held("v2_picked_scales", [P, S], U8)
+        nc.vector.tensor_copy(v2_picked_scales[:], v2_scales[:].indirect(list_v2[:]))
+        nc.vector.tensor_copy(v2_picked[:], v2_words[:].indirect(list_v2[:]))
+
+        d_codes = held("d_codes", [P, S], U32)
+        d_scales = held("d_scales", [P, S], U8)
+        for i in range(S // P):
+            cols = slice(i * P, (i + 1) * P)
+            bank = banks[4 + i]
+            for t in range(PACK):
+                nc.tensor.matmul_mx(
+                    out=bank[:, t * P:(t + 1) * P],
+                    lhsT=w2_dealt[:, t, :].bitcast(FP4X4), lhsT_scale=w2_dealt_scales[:, t, :],
+                    rhs=v2_picked[:, cols].bitcast(FP8X4), rhs_scale=v2_picked_scales[:, cols],
+                    start=True, stop=True,
+                )
+            silu = held("silu%d" % i, [P, P, PACK], F32)
+            nc.scalar.activation(silu[:], bank[:].rearrange("p (t s) -> p s t", t=PACK), ACT.Silu)
+            d_bf = held("d_bf%d" % i, [P, P, PACK], BF16)
+            nc.vector.tensor_tensor(d_bf[:], silu[:], g2_cols[:].unsqueeze(1).to_broadcast([P, P, PACK]), ALU.mult)
+            nc.vector.quantize_mx(
+                out=d_codes[:, cols].bitcast(FP8X4), scales=d_scales[:, cols], in_=d_bf[:].rearrange("p s t -> p (s t)")
+            )
+
+        v_picked = [held("v_picked%d" % a, [P, S], U32) for a in range(2)]
+        v_picked_scales = held("v_picked_scales", [P, S], U8)
+        nc.vector.tensor_copy(v_picked[0][:], v_words[0][:].indirect(list_v[:]))
+        nc.vector.tensor_copy(v_picked_scales[:], v_scales[:].indirect(list_v[:]))
+        nc.vector.tensor_copy(v_picked[1][:], v_words[1][:].indirect(list_v[:]))
+
+        res_sb = [shared("table", 3, "res%d" % half, [P, PACK, BANK], F32) for half in range(2)]
+        for half in range(2):
+            nc.sync.dma_start(out=res_sb[half][:], in_=res.rearrange("(p t) j -> p t j", t=PACK)[:, :, half * BANK:(half + 1) * BANK])
+
+        w_bf = [held("w_bf%d" % i, [P, 3, P, PACK], BF16) for i in range(2)]
+        w_codes = [held("w_codes%d" % c, [P, 3 * P], U32) for c in range(SLICES)]
+        w_scales = [held("w_scales%d" % c, [P, 3 * P], U8) for c in range(SLICES)]
+        tanh_sb = held("tanh_sb", [P, S], F32)
+        h1_sb = [held("h1_sb%d" % i, [P, S], F32) for i in range(2)]
+        h2_sb = [held("h2_sb%d" % i, [P, S], F32) for i in range(2)]
+        sum_turned = [[held("sum_turned%d_%d" % (i, half), [P, BANK], F32) for half in range(2)] for i in range(2)]
+        z_turned = [[held("z_turned%d_%d" % (a, half), [P, 4, 512], BF16) for half in range(2)] for a in range(2)]
+        z_codes = [held("z_codes%d" % a, [P, T2], U32) for a in range(2)]
+        z_scales = [held("z_scales%d" % a, [P, T2], U8) for a in range(2)]
+
+        def quantise_weights(c):
+            chunk, first = divmod(c * P, W_CHUNK)
+            for a in range(3):
+                nc.scalar.copy(
+                    out=w_bf[c % 2][:, a].rearrange("p (g i) t -> p g t i", i=4),
+                    in_=w_raw[chunk][a][:, :, first:first + P].rearrange("p t (g i) -> p g t i", i=4),
+                )
+            nc.vector.quantize_mx(
+                out=w_codes[c][:].bitcast(FP8X4), scales=w_scales[c][:],
+                in_=w_bf[c % 2][:].rearrange("p a w t -> p (a w t)"),
+            )
+
+        def features(c):
+            for a in range(2):
+                cols = slice(a * P, (a + 1) * P)
+                nc.tensor.matmul_mx(
+                    out=banks[0][:],
+                    lhsT=w_codes[c][:, cols].bitcast(FP8X4), lhsT_scale=w_scales[c][:, cols],
+                    rhs=v_picked[a][:].bitcast(FP8X4), rhs_scale=v_picked_scales[4 * a:P, :],
+                    start=(a == 0), stop=(a == 1),
+                )
+            nc.scalar.activation(tanh_sb[:], banks[0][:], ACT.Tanh)
+            nc.scalar.activation(h1_sb[c % 2][:], tanh_sb[:], ACT.Copy, scale=g1_cols[:, c:c + 1])
+            cols = slice(2 * P, 3 * P)
+            nc.tensor.matmul_mx(
+                out=banks[1][:],
+                lhsT=w_codes[c][:, cols].bitcast(FP8X4), lhsT_scale=w_scales[c][:, cols],
+                rhs=d_codes[:].bitcast(FP8X4), rhs_scale=d_scales[:],
+                start=True, stop=True,
+            )
+            nc.scalar.copy(out=h2_sb[c % 2][:], in_=banks[1][:])
+
+        def place(c):
+            nc.vector.tensor_tensor(pages_a[c % 2][:].indirect(list_pa[:]), h1_sb[c % 2][:], wg1_sb[:], ALU.mult)
+            nc.vector.tensor_tensor(pages_b[c % 2][:].indirect(list_pb[:]), h2_sb[c % 2][:], wg2_sb[:], ALU.mult)
+
+        def meet(c):
+            a, place_in_pass = divmod(c, 4)
+            for half in range(2):
+                bank = banks[2 + half]
+                for n, source in enumerate((cat_sb[c], pages_a[c % 2])):
+                    for j in range(4):
+                        first = half * BANK + j * P
+                        nc.tensor.matmul(
+                            bank[:, j * P:(j + 1) * P], source[:, first:first + P], ident[:],
+                            start=(n == 0 and j == 0), stop=(n == 1 and j == 3), is_transpose=True,
+                        )
+                nc.scalar.copy(out=sum_turned[c % 2][half][:], in_=bank[:])
+            for half in range(2):
+                bank = banks[4 + half]
+                for j in range(4):
+                    first = half * BANK + j * P
+                    nc.tensor.transpose(bank[:, j * P:(j + 1) * P], pages_b[c % 2][:, first:first + P], ident[:])
+                nc.vector.tensor_tensor(
+                    z_turned[a][half][:, :, place_in_pass * P:(place_in_pass + 1) * P],
+                    bank[:].rearrange("p (j r) -> p j r", j=4),
+                    sum_turned[c % 2][half][:].rearrange("p (j r) -> p j r", j=4),
+                    ALU.max,
+                )
+
+        def quantise_z(a, k):
+            bank = banks[6 + k % 2]
+            for j in range(2):
+                pairs = z_turned[a][k // 2][:, 2 * (k % 2) + j, :].bitcast(F32)
+                for u in range(2):
+                    first = (2 * j + u) * P
+                    nc.tensor.transpose(bank[:, first:first + P], pairs[:, u:2 * P:2], ident[:])
+            z_bf = shared("stage", 12, "z_bf%d_%d" % (a, k), [P, PACK * Y_CHUNK], BF16)
+            nc.scalar.copy(
+                out=z_bf[:].bitcast(F32).rearrange("p (j s u) -> p j s u", j=2, u=2),
+                in_=bank[:].rearrange("p (j u s) -> p j s u", j=2, u=2),
+            )
+            cols = slice(k * Y_CHUNK, (k + 1) * Y_CHUNK)
+            nc.vector.quantize_mx(out=z_codes[a][:, cols].bitcast(FP8X4), scales=z_scales[a][:, cols], in_=z_bf[:])
+
+        w4_dealt = held("w4_dealt", [P, 2, PACK, 2 * P], U8)
+        w4_dealt_scales = held("w4_dealt_scales", [P, 2, PACK, P], U8)
+
+        def deal_w4():
+            for a in range(2):
+                nc.vector.tensor_copy(
+                    out=w4_dealt[:, a].rearrange("p t (q b) -> p t q b", b=2),
+                    in_=w4_raw[:, a, :].rearrange("p (q t b) -> p t q b", t=PACK, b=2),
+                )
+            nc.vector.tensor_copy(out=w4_dealt_scales[:], in_=w4_raw_scales[:].rearrange("p a (q t) -> p a t q", t=PACK))
+
+        quantise_weights(0)
+        quantise_weights(1)
+        for c in range(SLICES + 1):
+            if c < SLICES:
+                features(c)
+                place(c)
+            if c + 2 < SLICES:
+                quantise_weights(c + 2)
+            if c > 0:
+                meet(c - 1)
+            if c == 5:
+                for k in range(T2 // Y_CHUNK):
+                    quantise_z(0, k)
+            if c == 6:
+                deal_w4()
+
+        y_codes = held("y_codes", [P, T2], U32)
+        y_scales = held("y_scales", [P, T2], U8)
+        out_rows = out_0.rearrange("(p t) j -> p t j", t=PACK)
+        out_words = words_of(out_1[0])
+
+        def finish(k):
+            cols = slice(k * Y_CHUNK, (k + 1) * Y_CHUNK)
+            y = shared("stage", 12, "y%d" % k, [P, PACK, Y_CHUNK], F32)
+            for pair in range(2):
+                bank = banks[2 * (k % 2) + pair]
+                for i in range(2):
+                    t = 2 * pair + i
+                    for a in range(2):
+                        nc.tensor.matmul_mx(
+                            out=bank[:, i * Y_CHUNK:(i + 1) * Y_CHUNK],
+                            lhsT=w4_dealt[:, a, t, :].bitcast(FP4X4), lhsT_scale=w4_dealt_scales[:, a, t, :],
+                            rhs=z_codes[a][:, cols].bitcast(FP8X4), rhs_scale=z_scales[a][:, cols],
+                            start=(a == 0), stop=(a == 1),
+                        )
+                nc.vector.tensor_tensor(
+                    y[:, 2 * pair:2 * pair + 2, :], bank[:].rearrange("p (i s) -> p i s", i=2),
+                    res_sb[k // 2][:, 2 * pair:2 * pair + 2, (k % 2) * Y_CHUNK:(k % 2 + 1) * Y_CHUNK], ALU.add,
+                )
+            nc.sync.dma_start(out=out_rows[:, :, cols], in_=y[:])
+            y_bf = shared("stage", 12, "y_bf%d" % k, [P, Y_CHUNK, PACK], BF16)
+            nc.scalar.copy(
+                out=y_bf[:].rearrange("p (g i) t -> p g t i", i=4),
+                in_=y[:].rearrange("p t (g i) -> p g t i", i=4),
+            )
+            nc.vector.quantize_mx(
+                out=y_codes[:, cols].bitcast(FP8X4), scales=y_scales[:, cols], in_=y_bf[:].rearrange("p s t -> p (s t)")
+            )
+            nc.sync.dma_start(out=out_words[:, cols], in_=y_codes[:, cols].bitcast(I32))
+
+        for k in range(T2 // Y_CHUNK + 1):
+            if k < T2 // Y_CHUNK:
+                quantise_z(1, k)
+            if k > 0:
+                finish(k - 1)
+        for q in range(4):
+            queue = nc.sync if q % 2 == 0 else nc.scalar
+            queue.dma_start(out=out_2[0, 4 * q:4 * q + 4, :].bitcast(I32), in_=y_scales[32 * q:32 * q + 4, :].bitcast(I32))

@@ -59,13 +59,14 @@ def tile_list_transit_vetting_pages_kernel(
         pages_a = [held("page_a%d" % i, [P, T2], F32) for i in range(2)]
         pages_b = [held("page_b%d" % i, [P, T2], F32) for i in range(2)]
 
-        for plane in (v2_scales, w2_raw_scales, v_scales):
-            nc.vector.memset(plane[:].bitcast(I32), 0)
-        nc.vector.memset(w4_raw_scales[:].rearrange("p a n -> p (a n)").bitcast(I32), 0)
+        for plane in (w2_raw_scales, v2_scales, v_scales):
+            nc.gpsimd.memset(plane[:].bitcast(I32), 0)
+        nc.gpsimd.memset(w4_raw_scales[:].rearrange("p a n -> p (a n)").bitcast(I32), 0)
         ident = held("ident", [P, P], F32)
         make_identity(nc, ident[:])
-        for page in (pages_a[0], pages_b[0], pages_a[1], pages_b[1]):
-            nc.gpsimd.memset(page[:], 0.0)
+        for i, engine in enumerate((nc.vector, nc.gpsimd)):
+            engine.memset(pages_a[i][:], 0.0)
+            engine.memset(pages_b[i][:], 0.0)
 
         g1_cols = held("g1_cols", [P, SLICES], F32)
         g2_cols = held("g2_cols", [P, PACK], F32)
@@ -78,45 +79,52 @@ def tile_list_transit_vetting_pages_kernel(
         def words_of(dram):
             return dram.rearrange("p t i -> p (t i)").bitcast(I32)
 
-        def load_weights(i):
+        def load_weights(i, parts):
             cols = slice(i * W_CHUNK, (i + 1) * W_CHUNK)
-            for a, rows in enumerate((w1[0:512, :], w1[512:1024, :], w3)):
+            for a in parts:
+                rows = (w1[0:512, :], w1[512:1024, :], w3)[a]
                 nc.sync.dma_start(out=w_raw[i][a][:], in_=rows.rearrange("(p j) w -> p j w", j=PACK)[:, :, cols])
 
         def load_cat(c):
             nc.sync.dma_start(out=cat_sb[c][:], in_=cat[c * P:(c + 1) * P, :])
 
+        nc.sync.dma_start(out=w2_raw[:].bitcast(I32), in_=w2_words[0].bitcast(I32))
+        nc.sync.dma_start(list_v2[:], offs2)
+        for q in range(4):
+            nc.sync.dma_start(out=w2_raw_scales[32 * q:32 * q + 4, :].bitcast(I32), in_=w2_scales[0, 4 * q:4 * q + 4, :].bitcast(I32))
         nc.sync.dma_start(out=v2_words[:].bitcast(I32), in_=words_of(tab2_words[0]))
         for q in range(4):
             nc.sync.dma_start(out=v2_scales[32 * q:32 * q + 4, :].bitcast(I32), in_=tab2_scales[0, 4 * q:4 * q + 4, :].bitcast(I32))
-        nc.sync.dma_start(list_v2[:], offs2)
-        nc.sync.dma_start(out=w2_raw[:].bitcast(I32), in_=w2_words[0].bitcast(I32))
-        nc.sync.dma_start(out=v_words[0][:].bitcast(I32), in_=words_of(tab_words[0]))
-        for q in range(4):
-            nc.sync.dma_start(out=w2_raw_scales[32 * q:32 * q + 4, :].bitcast(I32), in_=w2_scales[0, 4 * q:4 * q + 4, :].bitcast(I32))
         nc.sync.dma_start(list_v[:], offs)
+        nc.sync.dma_start(out=v_words[0][:].bitcast(I32), in_=words_of(tab_words[0]))
+        load_weights(0, (0,))
         nc.sync.dma_start(out=g2_cols[:], in_=g2.rearrange("(p t) -> p t", t=PACK))
-        nc.sync.dma_start(out=v_words[1][:].bitcast(I32), in_=words_of(tab_words[1]))
         for q in range(4):
             nc.sync.dma_start(out=v_scales[32 * q:32 * q + 8, :].bitcast(I32), in_=tab_scales[:, 4 * q:4 * q + 4, :].bitcast(I32))
-        load_weights(0)
-        with nc.allow_non_contiguous_dma(reason="one gain for each partition and slice"):
-            nc.sync.dma_start(out=g1_cols[:], in_=g1.rearrange("(c p) -> p c", p=P))
-        nc.sync.dma_start(out=wg1_sb[:], in_=wg1)
-        nc.sync.dma_start(list_pa[:], offs3)
-        nc.sync.dma_start(out=wg2_sb[:], in_=wg2)
-        nc.sync.dma_start(list_pb[:], offs4)
-        for i in range(1, n_chunks):
-            load_cat(i - 1)
-            load_weights(i)
-        load_cat(n_chunks - 1)
+        load_weights(0, (1,))
+        nc.sync.dma_start(out=v_words[1][:].bitcast(I32), in_=words_of(tab_words[1]))
         nc.sync.dma_start(out=w4_raw[:].bitcast(I32), in_=w4_words.rearrange("a p n -> p a n").bitcast(I32))
         for q in range(4):
             nc.sync.dma_start(
                 out=w4_raw_scales[32 * q:32 * q + 4, :, :].bitcast(I32),
                 in_=w4_scales[:, 4 * q:4 * q + 4, :].rearrange("a r n -> r a n").bitcast(I32),
             )
-        for c in range(n_chunks, SLICES):
+        load_weights(0, (2,))
+        with nc.allow_non_contiguous_dma(reason="one gain for each partition and slice"):
+            nc.sync.dma_start(out=g1_cols[:], in_=g1.rearrange("(c p) -> p c", p=P))
+        nc.sync.dma_start(out=wg1_sb[:], in_=wg1)
+        nc.sync.dma_start(list_pa[:], offs3)
+        load_weights(1, (0, 1, 2))
+        load_cat(0)
+        for u in range(2):
+            nc.sync.dma_start(out=wg2_sb[64 * u:64 * (u + 1), :], in_=wg2.rearrange("(q u e) s -> u q e s", u=2, e=2)[u])
+        nc.sync.dma_start(list_pb[:], offs4)
+        load_cat(1)
+        load_weights(2, (0, 1, 2))
+        load_cat(2)
+        load_cat(3)
+        load_weights(3, (0, 1, 2))
+        for c in range(4, SLICES):
             load_cat(c)
 
         w2_dealt = held("w2_dealt", [P, PACK, 2 * P], U8)
@@ -136,7 +144,7 @@ def tile_list_transit_vetting_pages_kernel(
         d_scales = held("d_scales", [P, S], U8)
         for i in range(S // P):
             cols = slice(i * P, (i + 1) * P)
-            bank = banks[4 + i]
+            bank = banks[(0, 7, 1, 2)[i]]
             for t in range(PACK):
                 nc.tensor.matmul_mx(
                     out=bank[:, t * P:(t + 1) * P],
@@ -162,57 +170,70 @@ def tile_list_transit_vetting_pages_kernel(
         for half in range(2):
             nc.sync.dma_start(out=res_sb[half][:], in_=res.rearrange("(p t) j -> p t j", t=PACK)[:, :, half * BANK:(half + 1) * BANK])
 
-        w_bf = [held("w_bf%d" % i, [P, 3, P, PACK], BF16) for i in range(2)]
-        w_codes = [held("w_codes%d" % c, [P, 3 * P], U32) for c in range(SLICES)]
-        w_scales = [held("w_scales%d" % c, [P, 3 * P], U8) for c in range(SLICES)]
-        tanh_sb = held("tanh_sb", [P, S], F32)
+        w1_bf = [held("w1_bf%d" % i, [P, 2, P, PACK], BF16) for i in range(2)]
+        w1_codes = [held("w1_codes%d" % c, [P, 2 * P], U32) for c in range(SLICES)]
+        w1_scales = [held("w1_scales%d" % c, [P, 2 * P], U8) for c in range(SLICES)]
+        w3_bf = held("w3_bf", [P, W_CHUNK, PACK], BF16)
+        w3_codes = [held("w3_codes%d" % i, [P, W_CHUNK], U32) for i in range(n_chunks)]
+        w3_scales = [held("w3_scales%d" % i, [P, W_CHUNK], U8) for i in range(n_chunks)]
         h1_sb = [held("h1_sb%d" % i, [P, S], F32) for i in range(2)]
         h2_sb = [held("h2_sb%d" % i, [P, S], F32) for i in range(2)]
         sum_turned = [[held("sum_turned%d_%d" % (i, half), [P, BANK], F32) for half in range(2)] for i in range(2)]
-        z_turned = [[held("z_turned%d_%d" % (a, half), [P, 4, 512], BF16) for half in range(2)] for a in range(2)]
+        z_turned = [[held("z_turned%d_%d" % (a, half), [P, 4, 2, 2 * P], BF16) for half in range(2)] for a in range(2)]
         z_codes = [held("z_codes%d" % a, [P, T2], U32) for a in range(2)]
         z_scales = [held("z_scales%d" % a, [P, T2], U8) for a in range(2)]
 
+        def round_and_interleave(out, in_):
+            nc.scalar.copy(out=out.rearrange("p (g i) t -> p g t i", i=4), in_=in_.rearrange("p t (g i) -> p g t i", i=4))
+
         def quantise_weights(c):
             chunk, first = divmod(c * P, W_CHUNK)
-            for a in range(3):
-                nc.scalar.copy(
-                    out=w_bf[c % 2][:, a].rearrange("p (g i) t -> p g t i", i=4),
-                    in_=w_raw[chunk][a][:, :, first:first + P].rearrange("p t (g i) -> p g t i", i=4),
-                )
+            for a in range(2):
+                round_and_interleave(w1_bf[c % 2][:, a], w_raw[chunk][a][:, :, first:first + P])
             nc.vector.quantize_mx(
-                out=w_codes[c][:].bitcast(FP8X4), scales=w_scales[c][:],
-                in_=w_bf[c % 2][:].rearrange("p a w t -> p (a w t)"),
+                out=w1_codes[c][:].bitcast(FP8X4), scales=w1_scales[c][:],
+                in_=w1_bf[c % 2][:].rearrange("p a w t -> p (a w t)"),
             )
+            if first == 0:
+                for first in range(0, W_CHUNK, P):
+                    nc.scalar.copy(
+                        out=w3_bf[:, first:first + P, :].rearrange("p (u q e) t -> p q t u e", u=2, e=2),
+                        in_=w_raw[chunk][2][:, :, first:first + P].rearrange("p t (q u e) -> p q t u e", u=2, e=2),
+                    )
+                nc.vector.quantize_mx(
+                    out=w3_codes[chunk][:].bitcast(FP8X4), scales=w3_scales[chunk][:],
+                    in_=w3_bf[:].rearrange("p w t -> p (w t)"),
+                )
 
         def features(c):
+            h2_bank, h1_bank = banks[3 + 2 * ((c - 1) % 2):][:2]
             for a in range(2):
                 cols = slice(a * P, (a + 1) * P)
                 nc.tensor.matmul_mx(
-                    out=banks[0][:],
-                    lhsT=w_codes[c][:, cols].bitcast(FP8X4), lhsT_scale=w_scales[c][:, cols],
+                    out=h1_bank[:],
+                    lhsT=w1_codes[c][:, cols].bitcast(FP8X4), lhsT_scale=w1_scales[c][:, cols],
                     rhs=v_picked[a][:].bitcast(FP8X4), rhs_scale=v_picked_scales[4 * a:P, :],
                     start=(a == 0), stop=(a == 1),
                 )
-            nc.scalar.activation(tanh_sb[:], banks[0][:], ACT.Tanh)
-            nc.scalar.activation(h1_sb[c % 2][:], tanh_sb[:], ACT.Copy, scale=g1_cols[:, c:c + 1])
-            cols = slice(2 * P, 3 * P)
+            nc.scalar.activation(h2_sb[c % 2][:], h1_bank[:], ACT.Tanh)
+            nc.scalar.activation(h1_sb[c % 2][:], h2_sb[c % 2][:], ACT.Copy, scale=g1_cols[:, c:c + 1])
+            chunk, first = divmod(c * P, W_CHUNK)
+            cols = slice(first, first + P)
             nc.tensor.matmul_mx(
-                out=banks[1][:],
-                lhsT=w_codes[c][:, cols].bitcast(FP8X4), lhsT_scale=w_scales[c][:, cols],
+                out=h2_bank[:],
+                lhsT=w3_codes[chunk][:, cols].bitcast(FP8X4), lhsT_scale=w3_scales[chunk][:, cols],
                 rhs=d_codes[:].bitcast(FP8X4), rhs_scale=d_scales[:],
                 start=True, stop=True,
             )
-            nc.scalar.copy(out=h2_sb[c % 2][:], in_=banks[1][:])
+            nc.scalar.copy(out=h2_sb[c % 2][:], in_=h2_bank[:])
 
         def place(c):
             nc.vector.tensor_tensor(pages_a[c % 2][:].indirect(list_pa[:]), h1_sb[c % 2][:], wg1_sb[:], ALU.mult)
             nc.vector.tensor_tensor(pages_b[c % 2][:].indirect(list_pb[:]), h2_sb[c % 2][:], wg2_sb[:], ALU.mult)
 
-        def meet(c):
-            a, place_in_pass = divmod(c, 4)
+        def turn_sum(c):
             for half in range(2):
-                bank = banks[2 + half]
+                bank = banks[(1 if c + 1 < SLICES else 5) + half]
                 for n, source in enumerate((cat_sb[c], pages_a[c % 2])):
                     for j in range(4):
                         first = half * BANK + j * P
@@ -220,26 +241,32 @@ def tile_list_transit_vetting_pages_kernel(
                             bank[:, j * P:(j + 1) * P], source[:, first:first + P], ident[:],
                             start=(n == 0 and j == 0), stop=(n == 1 and j == 3), is_transpose=True,
                         )
-                nc.scalar.copy(out=sum_turned[c % 2][half][:], in_=bank[:])
+                nc.scalar.copy(
+                    out=sum_turned[c % 2][half][:].rearrange("p (j u q e) -> p j u q e", j=4, u=2, e=2),
+                    in_=bank[:].rearrange("p (j q u e) -> p j u q e", j=4, u=2, e=2),
+                )
+
+        def maximum(c):
+            a, place_in_pass = divmod(c, 4)
             for half in range(2):
-                bank = banks[4 + half]
+                bank = banks[3 + 2 * (c % 2) + half]
                 for j in range(4):
                     first = half * BANK + j * P
                     nc.tensor.transpose(bank[:, j * P:(j + 1) * P], pages_b[c % 2][:, first:first + P], ident[:])
                 nc.vector.tensor_tensor(
-                    z_turned[a][half][:, :, place_in_pass * P:(place_in_pass + 1) * P],
-                    bank[:].rearrange("p (j r) -> p j r", j=4),
-                    sum_turned[c % 2][half][:].rearrange("p (j r) -> p j r", j=4),
+                    z_turned[a][half][:, :, :, place_in_pass * 64:(place_in_pass + 1) * 64],
+                    bank[:].rearrange("p (j u x) -> p j u x", j=4, u=2),
+                    sum_turned[c % 2][half][:].rearrange("p (j u x) -> p j u x", j=4, u=2),
                     ALU.max,
                 )
 
         def quantise_z(a, k):
-            bank = banks[6 + k % 2]
+            bank = banks[((0, 7), (3, 4))[a][k % 2]]
             for j in range(2):
-                pairs = z_turned[a][k // 2][:, 2 * (k % 2) + j, :].bitcast(F32)
                 for u in range(2):
                     first = (2 * j + u) * P
-                    nc.tensor.transpose(bank[:, first:first + P], pairs[:, u:2 * P:2], ident[:])
+                    pairs = z_turned[a][k // 2][:, 2 * (k % 2) + j, u, :].bitcast(F32)
+                    nc.tensor.transpose(bank[:, first:first + P], pairs, ident[:])
             z_bf = shared("stage", 12, "z_bf%d_%d" % (a, k), [P, PACK * Y_CHUNK], BF16)
             nc.scalar.copy(
                 out=z_bf[:].bitcast(F32).rearrange("p (j s u) -> p j s u", j=2, u=2),
@@ -259,61 +286,72 @@ def tile_list_transit_vetting_pages_kernel(
                 )
             nc.vector.tensor_copy(out=w4_dealt_scales[:], in_=w4_raw_scales[:].rearrange("p a (q t) -> p a t q", t=PACK))
 
-        quantise_weights(0)
-        quantise_weights(1)
-        for c in range(SLICES + 1):
-            if c < SLICES:
-                features(c)
-                place(c)
-            if c + 2 < SLICES:
-                quantise_weights(c + 2)
-            if c > 0:
-                meet(c - 1)
-            if c == 5:
-                for k in range(T2 // Y_CHUNK):
-                    quantise_z(0, k)
-            if c == 6:
-                deal_w4()
-
         y_codes = held("y_codes", [P, T2], U32)
         y_scales = held("y_scales", [P, T2], U8)
         out_rows = out_0.rearrange("(p t) j -> p t j", t=PACK)
         out_words = words_of(out_1[0])
+        y_banks = ((0, 7), (1, 2), (5, 6), (0, 7))
+
+        def last_product(a, k):
+            cols = slice(k * Y_CHUNK, (k + 1) * Y_CHUNK)
+            for t in range(PACK):
+                pair, i = divmod(t, 2)
+                nc.tensor.matmul_mx(
+                    out=banks[y_banks[k][pair]][:, i * Y_CHUNK:(i + 1) * Y_CHUNK],
+                    lhsT=w4_dealt[:, a, t, :].bitcast(FP4X4), lhsT_scale=w4_dealt_scales[:, a, t, :],
+                    rhs=z_codes[a][:, cols].bitcast(FP8X4), rhs_scale=z_scales[a][:, cols],
+                    start=(a == 0 and i == 0), stop=(a == 1 and i == 1),
+                )
 
         def finish(k):
             cols = slice(k * Y_CHUNK, (k + 1) * Y_CHUNK)
             y = shared("stage", 12, "y%d" % k, [P, PACK, Y_CHUNK], F32)
+            last_product(1, k)
             for pair in range(2):
-                bank = banks[2 * (k % 2) + pair]
-                for i in range(2):
-                    t = 2 * pair + i
-                    for a in range(2):
-                        nc.tensor.matmul_mx(
-                            out=bank[:, i * Y_CHUNK:(i + 1) * Y_CHUNK],
-                            lhsT=w4_dealt[:, a, t, :].bitcast(FP4X4), lhsT_scale=w4_dealt_scales[:, a, t, :],
-                            rhs=z_codes[a][:, cols].bitcast(FP8X4), rhs_scale=z_scales[a][:, cols],
-                            start=(a == 0), stop=(a == 1),
-                        )
                 nc.vector.tensor_tensor(
-                    y[:, 2 * pair:2 * pair + 2, :], bank[:].rearrange("p (i s) -> p i s", i=2),
+                    y[:, 2 * pair:2 * pair + 2, :], banks[y_banks[k][pair]][:].rearrange("p (i s) -> p i s", i=2),
                     res_sb[k // 2][:, 2 * pair:2 * pair + 2, (k % 2) * Y_CHUNK:(k % 2 + 1) * Y_CHUNK], ALU.add,
                 )
             nc.sync.dma_start(out=out_rows[:, :, cols], in_=y[:])
             y_bf = shared("stage", 12, "y_bf%d" % k, [P, Y_CHUNK, PACK], BF16)
-            nc.scalar.copy(
-                out=y_bf[:].rearrange("p (g i) t -> p g t i", i=4),
-                in_=y[:].rearrange("p t (g i) -> p g t i", i=4),
-            )
+            if k + 1 < T2 // Y_CHUNK:
+                round_and_interleave(y_bf[:], y[:])
+            else:
+                nc.vector.tensor_copy(
+                    out=y_bf[:].rearrange("p (g i) t -> p g t i", i=4), in_=y[:].rearrange("p t (g i) -> p g t i", i=4)
+                )
             nc.vector.quantize_mx(
                 out=y_codes[:, cols].bitcast(FP8X4), scales=y_scales[:, cols], in_=y_bf[:].rearrange("p s t -> p (s t)")
             )
             nc.sync.dma_start(out=out_words[:, cols], in_=y_codes[:, cols].bitcast(I32))
 
-        for k in range(T2 // Y_CHUNK + 1):
-            if k < T2 // Y_CHUNK:
-                quantise_z(1, k)
-            if k > 0:
-                finish(k - 1)
+        quantise_weights(0)
+        quantise_weights(1)
+        deal_w4()
+        for c in range(SLICES):
+            features(c)
+            place(c)
+            if c + 2 < SLICES:
+                quantise_weights(c + 2)
+            if c > 0:
+                turn_sum(c - 1)
+                maximum(c - 1)
+            for k in {5: (0,), 6: (1,), 7: (2, 3)}.get(c, ()):
+                quantise_z(0, k)
+        last_product(0, 0)
+        turn_sum(SLICES - 1)
+        last_product(0, 1)
+        maximum(SLICES - 1)
+        quantise_z(1, 0)
+        quantise_z(1, 1)
+        finish(0)
+        quantise_z(1, 2)
+        finish(1)
+        quantise_z(1, 3)
+        last_product(0, 2)
+        finish(2)
+        last_product(0, 3)
+        finish(3)
         for q in range(4):
             queue = nc.sync if q % 2 == 0 else nc.scalar
             queue.dma_start(out=out_2[0, 4 * q:4 * q + 4, :].bitcast(I32), in_=y_scales[32 * q:32 * q + 4, :].bitcast(I32))

@@ -102,6 +102,9 @@ def tile_list_transit_vetting_pages_kernel(
         for q in range(4):
             nc.sync.dma_start(out=v_scales[32 * q:32 * q + 8, :].bitcast(I32), in_=tab_scales[:, 4 * q:4 * q + 4, :].bitcast(I32))
         load_weights(0, (1,))
+        load_weights(0, (2,))
+        with nc.allow_non_contiguous_dma(reason="one gain for each partition and slice"):
+            nc.sync.dma_start(out=g1_cols[:], in_=g1.rearrange("(c p) -> p c", p=P))
         nc.sync.dma_start(out=v_words[1][:].bitcast(I32), in_=words_of(tab_words[1]))
         nc.sync.dma_start(out=w4_raw[:].bitcast(I32), in_=w4_words.rearrange("a p n -> p a n").bitcast(I32))
         for q in range(4):
@@ -109,9 +112,6 @@ def tile_list_transit_vetting_pages_kernel(
                 out=w4_raw_scales[32 * q:32 * q + 4, :, :].bitcast(I32),
                 in_=w4_scales[:, 4 * q:4 * q + 4, :].rearrange("a r n -> r a n").bitcast(I32),
             )
-        load_weights(0, (2,))
-        with nc.allow_non_contiguous_dma(reason="one gain for each partition and slice"):
-            nc.sync.dma_start(out=g1_cols[:], in_=g1.rearrange("(c p) -> p c", p=P))
         nc.sync.dma_start(out=wg1_sb[:], in_=wg1)
         nc.sync.dma_start(list_pa[:], offs3)
         load_weights(1, (0, 1, 2))
@@ -178,7 +178,7 @@ def tile_list_transit_vetting_pages_kernel(
         w3_scales = [held("w3_scales%d" % i, [P, W_CHUNK], U8) for i in range(n_chunks)]
         h1_sb = [held("h1_sb%d" % i, [P, S], F32) for i in range(2)]
         h2_sb = [held("h2_sb%d" % i, [P, S], F32) for i in range(2)]
-        sum_turned = [[held("sum_turned%d_%d" % (i, half), [P, BANK], F32) for half in range(2)] for i in range(2)]
+        sum_turned = [[shared("sum%d_%d" % (i, half), 1, "sum_turned%d_%d" % (i, half), [P, BANK], F32) for half in range(2)] for i in range(2)]
         z_turned = [[held("z_turned%d_%d" % (a, half), [P, 4, 2, 2 * P], BF16) for half in range(2)] for a in range(2)]
         z_codes = [held("z_codes%d" % a, [P, T2], U32) for a in range(2)]
         z_scales = [held("z_scales%d" % a, [P, T2], U8) for a in range(2)]
@@ -260,37 +260,42 @@ def tile_list_transit_vetting_pages_kernel(
                     ALU.max,
                 )
 
+        z_bf = {}
+
         def quantise_z(a, k):
-            bank = banks[((0, 7), (3, 4))[a][k % 2]]
+            bank = banks[((0, 7, 0, 7), (3, 4, 5, 6))[a][k]]
             for j in range(2):
                 for u in range(2):
                     first = (2 * j + u) * P
                     pairs = z_turned[a][k // 2][:, 2 * (k % 2) + j, u, :].bitcast(F32)
                     nc.tensor.transpose(bank[:, first:first + P], pairs, ident[:])
-            z_bf = shared("stage", 12, "z_bf%d_%d" % (a, k), [P, PACK * Y_CHUNK], BF16)
+            group = 2 - a
+            if k % group == 0:
+                z_bf[a] = shared("stage", 12, "z_bf%d_%d" % (a, k), [P, group * PACK * Y_CHUNK], BF16)
+            part = slice(k % group * PACK * Y_CHUNK, (k % group + 1) * PACK * Y_CHUNK)
             nc.scalar.copy(
-                out=z_bf[:].bitcast(F32).rearrange("p (j s u) -> p j s u", j=2, u=2),
+                out=z_bf[a][:, part].bitcast(F32).rearrange("p (j s u) -> p j s u", j=2, u=2),
                 in_=bank[:].rearrange("p (j u s) -> p j s u", j=2, u=2),
             )
-            cols = slice(k * Y_CHUNK, (k + 1) * Y_CHUNK)
-            nc.vector.quantize_mx(out=z_codes[a][:, cols].bitcast(FP8X4), scales=z_scales[a][:, cols], in_=z_bf[:])
+            if (k + 1) % group == 0:
+                cols = slice((k + 1 - group) * Y_CHUNK, (k + 1) * Y_CHUNK)
+                nc.vector.quantize_mx(out=z_codes[a][:, cols].bitcast(FP8X4), scales=z_scales[a][:, cols], in_=z_bf[a][:])
 
-        w4_dealt = held("w4_dealt", [P, 2, PACK, 2 * P], U8)
+        w4_dealt = {}
         w4_dealt_scales = held("w4_dealt_scales", [P, 2, PACK, P], U8)
 
-        def deal_w4():
-            for a in range(2):
-                nc.vector.tensor_copy(
-                    out=w4_dealt[:, a].rearrange("p t (q b) -> p t q b", b=2),
-                    in_=w4_raw[:, a, :].rearrange("p (q t b) -> p t q b", t=PACK, b=2),
-                )
-            nc.vector.tensor_copy(out=w4_dealt_scales[:], in_=w4_raw_scales[:].rearrange("p a (q t) -> p a t q", t=PACK))
+        def deal_w4_words(a, tile):
+            w4_dealt[a] = tile
+            nc.vector.tensor_copy(
+                out=tile[:].rearrange("p t (q b) -> p t q b", b=2),
+                in_=w4_raw[:, a, :].rearrange("p (q t b) -> p t q b", t=PACK, b=2),
+            )
 
         y_codes = held("y_codes", [P, T2], U32)
         y_scales = held("y_scales", [P, T2], U8)
         out_rows = out_0.rearrange("(p t) j -> p t j", t=PACK)
         out_words = words_of(out_1[0])
-        y_banks = ((0, 7), (1, 2), (5, 6), (0, 7))
+        y_banks = ((0, 7), (1, 2), (3, 4), (5, 6))
 
         def last_product(a, k):
             cols = slice(k * Y_CHUNK, (k + 1) * Y_CHUNK)
@@ -298,7 +303,7 @@ def tile_list_transit_vetting_pages_kernel(
                 pair, i = divmod(t, 2)
                 nc.tensor.matmul_mx(
                     out=banks[y_banks[k][pair]][:, i * Y_CHUNK:(i + 1) * Y_CHUNK],
-                    lhsT=w4_dealt[:, a, t, :].bitcast(FP4X4), lhsT_scale=w4_dealt_scales[:, a, t, :],
+                    lhsT=w4_dealt[a][:, t, :].bitcast(FP4X4), lhsT_scale=w4_dealt_scales[:, a, t, :],
                     rhs=z_codes[a][:, cols].bitcast(FP8X4), rhs_scale=z_scales[a][:, cols],
                     start=(a == 0 and i == 0), stop=(a == 1 and i == 1),
                 )
@@ -327,7 +332,8 @@ def tile_list_transit_vetting_pages_kernel(
 
         quantise_weights(0)
         quantise_weights(1)
-        deal_w4()
+        deal_w4_words(0, held("w4_dealt0", [P, PACK, 2 * P], U8))
+        nc.vector.tensor_copy(out=w4_dealt_scales[:], in_=w4_raw_scales[:].rearrange("p a (q t) -> p a t q", t=PACK))
         for c in range(SLICES):
             features(c)
             place(c)
@@ -342,16 +348,14 @@ def tile_list_transit_vetting_pages_kernel(
         turn_sum(SLICES - 1)
         last_product(0, 1)
         maximum(SLICES - 1)
-        quantise_z(1, 0)
-        quantise_z(1, 1)
+        deal_w4_words(1, shared("sum1_1", 1, "w4_dealt1", [P, PACK, 2 * P], U8))
+        for k in range(T2 // Y_CHUNK):
+            quantise_z(1, k)
         finish(0)
-        quantise_z(1, 2)
         finish(1)
-        quantise_z(1, 3)
-        last_product(0, 2)
-        finish(2)
-        last_product(0, 3)
-        finish(3)
+        for k in (2, 3):
+            last_product(0, k)
+            finish(k)
         for q in range(4):
             queue = nc.sync if q % 2 == 0 else nc.scalar
             queue.dma_start(out=out_2[0, 4 * q:4 * q + 4, :].bitcast(I32), in_=y_scales[32 * q:32 * q + 4, :].bitcast(I32))

@@ -64,9 +64,8 @@ def tile_list_transit_vetting_pages_kernel(
         nc.gpsimd.memset(w4_raw_scales[:].rearrange("p a n -> p (a n)").bitcast(I32), 0)
         ident = held("ident", [P, P], F32)
         make_identity(nc, ident[:])
-        for i, engine in enumerate((nc.vector, nc.gpsimd)):
-            engine.memset(pages_a[i][:], 0.0)
-            engine.memset(pages_b[i][:], 0.0)
+        for page in pages_a + pages_b:
+            nc.vector.memset(page[:], 0.0)
 
         g1_cols = held("g1_cols", [P, SLICES], F32)
         g2_cols = held("g2_cols", [P, PACK], F32)
@@ -97,10 +96,10 @@ def tile_list_transit_vetting_pages_kernel(
             nc.sync.dma_start(out=v2_scales[32 * q:32 * q + 4, :].bitcast(I32), in_=tab2_scales[0, 4 * q:4 * q + 4, :].bitcast(I32))
         nc.sync.dma_start(list_v[:], offs)
         nc.sync.dma_start(out=v_words[0][:].bitcast(I32), in_=words_of(tab_words[0]))
-        load_weights(0, (0,))
-        nc.sync.dma_start(out=g2_cols[:], in_=g2.rearrange("(p t) -> p t", t=PACK))
         for q in range(4):
             nc.sync.dma_start(out=v_scales[32 * q:32 * q + 8, :].bitcast(I32), in_=tab_scales[:, 4 * q:4 * q + 4, :].bitcast(I32))
+        nc.sync.dma_start(out=g2_cols[:], in_=g2.rearrange("(p t) -> p t", t=PACK))
+        load_weights(0, (0,))
         load_weights(0, (1,))
         load_weights(0, (2,))
         with nc.allow_non_contiguous_dma(reason="one gain for each partition and slice"):
@@ -317,7 +316,7 @@ def tile_list_transit_vetting_pages_kernel(
                     y[:, 2 * pair:2 * pair + 2, :], banks[y_banks[k][pair]][:].rearrange("p (i s) -> p i s", i=2),
                     res_sb[k // 2][:, 2 * pair:2 * pair + 2, (k % 2) * Y_CHUNK:(k % 2 + 1) * Y_CHUNK], ALU.add,
                 )
-            nc.sync.dma_start(out=out_rows[:, :, cols], in_=y[:])
+                nc.sync.dma_start(out=out_rows[:, 2 * pair:2 * pair + 2, cols], in_=y[:, 2 * pair:2 * pair + 2, :])
             y_bf = shared("stage", 12, "y_bf%d" % k, [P, Y_CHUNK, PACK], BF16)
             if k + 1 < T2 // Y_CHUNK:
                 round_and_interleave(y_bf[:], y[:])
@@ -328,7 +327,6 @@ def tile_list_transit_vetting_pages_kernel(
             nc.vector.quantize_mx(
                 out=y_codes[:, cols].bitcast(FP8X4), scales=y_scales[:, cols], in_=y_bf[:].rearrange("p s t -> p (s t)")
             )
-            nc.sync.dma_start(out=out_words[:, cols], in_=y_codes[:, cols].bitcast(I32))
 
         quantise_weights(0)
         quantise_weights(1)
@@ -356,6 +354,8 @@ def tile_list_transit_vetting_pages_kernel(
         for k in (2, 3):
             last_product(0, k)
             finish(k)
+        for cols in (slice(0, T2 - Y_CHUNK), slice(T2 - Y_CHUNK, T2)):
+            nc.sync.dma_start(out=out_words[:, cols], in_=y_codes[:, cols].bitcast(I32))
         for q in range(4):
             queue = nc.sync if q % 2 == 0 else nc.scalar
             queue.dma_start(out=out_2[0, 4 * q:4 * q + 4, :].bitcast(I32), in_=y_scales[32 * q:32 * q + 4, :].bitcast(I32))

@@ -62,6 +62,8 @@ def tile_list_transit_vetting_pages_kernel(
         for plane in (w2_raw_scales, v2_scales, v_scales):
             nc.gpsimd.memset(plane[:].bitcast(I32), 0)
         nc.gpsimd.memset(w4_raw_scales[:].rearrange("p a n -> p (a n)").bitcast(I32), 0)
+        g1_rows = held("g1_rows", [P, P], F32)
+        nc.gpsimd.memset(g1_rows[:], 0.0)
         ident = held("ident", [P, P], F32)
         make_identity(nc, ident[:])
         for page in pages_a + pages_b:
@@ -102,8 +104,7 @@ def tile_list_transit_vetting_pages_kernel(
         load_weights(0, (0,))
         load_weights(0, (1,))
         load_weights(0, (2,))
-        with nc.allow_non_contiguous_dma(reason="one gain for each partition and slice"):
-            nc.sync.dma_start(out=g1_cols[:], in_=g1.rearrange("(c p) -> p c", p=P))
+        nc.sync.dma_start(out=g1_rows[0:SLICES, :], in_=g1.rearrange("(c p) -> c p", p=P))
         nc.sync.dma_start(out=v_words[1][:].bitcast(I32), in_=words_of(tab_words[1]))
         nc.sync.dma_start(out=w4_raw[:].bitcast(I32), in_=w4_words.rearrange("a p n -> p a n").bitcast(I32))
         for q in range(4):
@@ -158,6 +159,9 @@ def tile_list_transit_vetting_pages_kernel(
             nc.vector.quantize_mx(
                 out=d_codes[:, cols].bitcast(FP8X4), scales=d_scales[:, cols], in_=d_bf[:].rearrange("p s t -> p (s t)")
             )
+
+        nc.tensor.transpose(banks[3][:, 0:P], g1_rows[:], ident[:])
+        nc.scalar.copy(out=g1_cols[:], in_=banks[3][:, 0:SLICES])
 
         v_picked = [held("v_picked%d" % a, [P, S], U32) for a in range(2)]
         v_picked_scales = held("v_picked_scales", [P, S], U8)

from contextlib import ExitStack

import concourse.mybir as mybir
from concourse.masks import make_identity

F32 = mybir.dt.float32
BF16 = mybir.dt.bfloat16
I32 = mybir.dt.int32
U32 = mybir.dt.uint32
U16 = mybir.dt.uint16
U8 = mybir.dt.uint8
FP8X4 = mybir.dt.float8_e4m3fn_x4
FP4X4 = mybir.dt.float4_e2m1fn_x4
ACT = mybir.ActivationFunctionType
ALU = mybir.AluOpType

T, S, K, K2, M, H, N, T2 = 2048, 512, 1024, 512, 512, 1024, 512, 1024
FLOPS = 2 * S * (K * H + K2 * M + M * H) + 2 * H * N * T2

P = 128
PACK = 4
BANK = 512
SLICES = H // P
W_CHUNK = 256
Y_CHUNK = 256


def tile_list_transit_vetting_pages_kernel(
    tc, tab_words, tab_scales, tab2_words, tab2_scales, offs, offs2, offs3, offs4,
    w1, g1, w2_words, w2_scales, g2, w3, wg1, wg2, cat, w4_words, w4_scales, res,
    out_0, out_1, out_2,
):
    nc = tc.nc
    with ExitStack() as ctx:
        sb = ctx.enter_context(tc.tile_pool(name="sb", bufs=1))
        ps = ctx.enter_context(tc.psum_pool(name="ps", bufs=1))

        def held(name, shape, dtype):
            return sb.tile(shape, dtype, name=name, align_bytes=64)

        def shared(tag, bufs, name, shape, dtype):
            return sb.tile(shape, dtype, name=name, tag=tag, bufs=bufs, align_bytes=64)

        banks = [ps.tile([P, BANK], F32, name="bank%d" % b) for b in range(8)]

        list_v = held("list_v", [P, S // 16], U16)
        list_v2 = held("list_v2", [P, S // 16], U16)
        list_pa = held("list_pa", [P, S // 16], U16)
        list_pb = held("list_pb", [P, S // 16], U16)

        v_words = [shared("table", 3, "v_words%d" % a, [P, T], U32) for a in range(2)]
        v_scales = held("v_scales", [P, T], U8)
        v2_words = shared("table", 3, "v2_words", [P, T], U32)
        v2_scales = held("v2_scales", [P, T], U8)
        w2_raw = held("w2_raw", [P, 2 * M], U8)
        w2_raw_scales = held("w2_raw_scales", [P, M], U8)
        w4_raw = held("w4_raw", [P, 2, 2 * N], U8)
        w4_raw_scales = held("w4_raw_scales", [P, 2, N], U8)
        pages_a = [held("page_a%d" % i, [P, T2], F32) for i in range(2)]
        pages_b = [held("page_b%d" % i, [P, T2], F32) for i in range(2)]

        for plane in (w2_raw_scales, v2_scales, v_scales):
            nc.gpsimd.memset(plane[:].bitcast(I32), 0)
        nc.gpsimd.memset(w4_raw_scales[:].rearrange("p a n -> p (a n)").bitcast(I32), 0)
        g1_rows = held("g1_rows", [P, P], F32)
        nc.gpsimd.memset(g1_rows[:], 0.0)
        ident = held("ident", [P, P], F32)
        make_identity(nc, ident[:])
        for page in pages_a + pages_b:
            nc.vector.memset(page[:], 0.0)

        g1_cols = held("g1_cols", [P, SLICES], F32)
        g2_cols = held("g2_cols", [P, PACK], F32)
        wg1_sb = held("wg1_sb", [P, S], F32)
        wg2_sb = held("wg2_sb", [P, S], F32)
        n_chunks = H // W_CHUNK
        w_raw = [[shared("stage", 12, "w_raw%d_%d" % (i, a), [P, PACK, W_CHUNK], F32) for a in range(3)] for i in range(n_chunks)]
        cat_sb = [held("cat%d" % c, [P, T2], F32) for c in range(SLICES)]

        def words_of(dram):
            return dram.rearrange("p t i -> p (t i)").bitcast(I32)

        def load_weights(i, parts):
            cols = slice(i * W_CHUNK, (i + 1) * W_CHUNK)
            for a in parts:
                rows = (w1[0:512, :], w1[512:1024, :], w3)[a]
                nc.sync.dma_start(out=w_raw[i][a][:], in_=rows.rearrange("(p j) w -> p j w", j=PACK)[:, :, cols])

        def load_cat(c):
            nc.sync.dma_start(out=cat_sb[c][:], in_=cat[c * P:(c + 1) * P, :])

        nc.sync.dma_start(out=w2_raw[:].bitcast(I32), in_=w2_words[0].bitcast(I32))
        nc.sync.dma_start(list_v2[:], offs2)
        for q in range(4):
            nc.sync.dma_start(out=w2_raw_scales[32 * q:32 * q + 4, :].bitcast(I32), in_=w2_scales[0, 4 * q:4 * q + 4, :].bitcast(I32))
        nc.sync.dma_start(out=v2_words[:].bitcast(I32), in_=words_of(tab2_words[0]))
        for q in range(4):
            nc.sync.dma_start(out=v2_scales[32 * q:32 * q + 4, :].bitcast(I32), in_=tab2_scales[0, 4 * q:4 * q + 4, :].bitcast(I32))
        nc.sync.dma_start(list_v[:], offs)
        nc.sync.dma_start(out=v_words[0][:].bitcast(I32), in_=words_of(tab_words[0]))
        for q in range(4):
            nc.sync.dma_start(out=v_scales[32 * q:32 * q + 8, :].bitcast(I32), in_=tab_scales[:, 4 * q:4 * q + 4, :].bitcast(I32))
        nc.sync.dma_start(out=g2_cols[:], in_=g2.rearrange("(p t) -> p t", t=PACK))
        load_weights(0, (0,))
        load_weights(0, (1,))
        load_weights(0, (2,))
        nc.sync.dma_start(out=g1_rows[0:SLICES, :], in_=g1.rearrange("(c p) -> c p", p=P))
        nc.sync.dma_start(out=v_words[1][:].bitcast(I32), in_=words_of(tab_words[1]))
        nc.sync.dma_start(out=w4_raw[:].bitcast(I32), in_=w4_words.rearrange("a p n -> p a n").bitcast(I32))
        for q in range(4):
            nc.sync.dma_start(
                out=w4_raw_scales[32 * q:32 * q + 4, :, :].bitcast(I32),
                in_=w4_scales[:, 4 * q:4 * q + 4, :].rearrange("a r n -> r a n").bitcast(I32),
            )
        nc.sync.dma_start(out=wg1_sb[:], in_=wg1)
        nc.sync.dma_start(list_pa[:], offs3)
        load_weights(1, (0, 1, 2))
        load_cat(0)
        for u in range(2):
            nc.sync.dma_start(out=wg2_sb[64 * u:64 * (u + 1), :], in_=wg2.rearrange("(q u e) s -> u q e s", u=2, e=2)[u])
        nc.sync.dma_start(list_pb[:], offs4)
        load_cat(1)
        load_weights(2, (0, 1, 2))
        load_cat(2)
        load_cat(3)
        load_weights(3, (0, 1, 2))
        for c in range(4, SLICES):
            load_cat(c)

        w2_dealt = held("w2_dealt", [P, PACK, 2 * P], U8)
        w2_dealt_scales = held("w2_dealt_scales", [P, PACK, P], U8)
        nc.vector.tensor_copy(
            out=w2_dealt[:].rearrange("p t (q b) -> p t q b", b=2),
            in_=w2_raw[:].rearrange("p (q t b) -> p t q b", t=PACK, b=2),
        )
        nc.vector.tensor_copy(out=w2_dealt_scales[:], in_=w2_raw_scales[:].rearrange("p (q t) -> p t q", t=PACK))

        v2_picked = held("v2_picked", [P, S], U32)
        v2_picked_scales = held("v2_picked_scales", [P, S], U8)
        nc.vector.tensor_copy(v2_picked_scales[:], v2_scales[:].indirect(list_v2[:]))
        nc.vector.tensor_copy(v2_picked[:], v2_words[:].indirect(list_v2[:]))

        d_codes = held("d_codes", [P, S], U32)
        d_scales = held("d_scales", [P, S], U8)
        for i in range(S // P):
            cols = slice(i * P, (i + 1) * P)
            bank = banks[(0, 7, 1, 2)[i]]
            for t in range(PACK):
                nc.tensor.matmul_mx(
                    out=bank[:, t * P:(t + 1) * P],
                    lhsT=w2_dealt[:, t, :].bitcast(FP4X4), lhsT_scale=w2_dealt_scales[:, t, :],
                    rhs=v2_picked[:, cols].bitcast(FP8X4), rhs_scale=v2_picked_scales[:, cols],
                    start=True, stop=True,
                )
            silu = held("silu%d" % i, [P, P, PACK], F32)
            nc.scalar.activation(silu[:], bank[:].rearrange("p (t s) -> p s t", t=PACK), ACT.Silu)
            d_bf = held("d_bf%d" % i, [P, P, PACK], BF16)
            nc.vector.tensor_tensor(d_bf[:], silu[:], g2_cols[:].unsqueeze(1).to_broadcast([P, P, PACK]), ALU.mult)
            nc.vector.quantize_mx(
                out=d_codes[:, cols].bitcast(FP8X4), scales=d_scales[:, cols], in_=d_bf[:].rearrange("p s t -> p (s t)")
            )

        nc.tensor.transpose(banks[3][:, 0:P], g1_rows[:], ident[:])
        nc.scalar.copy(out=g1_cols[:], in_=banks[3][:, 0:SLICES])

        v_picked = [held("v_picked%d" % a, [P, S], U32) for a in range(2)]
        v_picked_scales = held("v_picked_scales", [P, S], U8)
        nc.vector.tensor_copy(v_picked[0][:], v_words[0][:].indirect(list_v[:]))
        nc.vector.tensor_copy(v_picked_scales[:], v_scales[:].indirect(list_v[:]))
        nc.vector.tensor_copy(v_picked[1][:], v_words[1][:].indirect(list_v[:]))

        res_sb = [shared("table", 3, "res%d" % half, [P, PACK, BANK], F32) for half in range(2)]
        for half in range(2):
            nc.sync.dma_start(out=res_sb[half][:], in_=res.rearrange("(p t) j -> p t j", t=PACK)[:, :, half * BANK:(half + 1) * BANK])

        w1_bf = [held("w1_bf%d" % i, [P, 2, P, PACK], BF16) for i in range(2)]
        w1_codes = [held("w1_codes%d" % c, [P, 2 * P], U32) for c in range(SLICES)]
        w1_scales = [held("w1_scales%d" % c, [P, 2 * P], U8) for c in range(SLICES)]
        w3_bf = held("w3_bf", [P, W_CHUNK, PACK], BF16)
        w3_codes = [held("w3_codes%d" % i, [P, W_CHUNK], U32) for i in range(n_chunks)]
        w3_scales = [held("w3_scales%d" % i, [P, W_CHUNK], U8) for i in range(n_chunks)]
        h1_sb = [held("h1_sb%d" % i, [P, S], F32) for i in range(2)]
        h2_sb = [held("h2_sb%d" % i, [P, S], F32) for i in range(2)]
        sum_turned = [[shared("sum%d_%d" % (i, half), 1, "sum_turned%d_%d" % (i, half), [P, BANK], F32) for half in range(2)] for i in range(2)]
        z_turned = [[held("z_turned%d_%d" % (a, half), [P, 4, 2, 2 * P], BF16) for half in range(2)] for a in range(2)]
        z_codes = [held("z_codes%d" % a, [P, T2], U32) for a in range(2)]
        z_scales = [held("z_scales%d" % a, [P, T2], U8) for a in range(2)]

        def round_and_interleave(out, in_):
            nc.scalar.copy(out=out.rearrange("p (g i) t -> p g t i", i=4), in_=in_.rearrange("p t (g i) -> p g t i", i=4))

        def quantise_weights(c):
            chunk, first = divmod(c * P, W_CHUNK)
            for a in range(2):
                round_and_interleave(w1_bf[c % 2][:, a], w_raw[chunk][a][:, :, first:first + P])
            nc.vector.quantize_mx(
                out=w1_codes[c][:].bitcast(FP8X4), scales=w1_scales[c][:],
                in_=w1_bf[c % 2][:].rearrange("p a w t -> p (a w t)"),
            )
            if first == 0:
                for first in range(0, W_CHUNK, P):
                    nc.scalar.copy(
                        out=w3_bf[:, first:first + P, :].rearrange("p (u q e) t -> p q t u e", u=2, e=2),
                        in_=w_raw[chunk][2][:, :, first:first + P].rearrange("p t (q u e) -> p q t u e", u=2, e=2),
                    )
                nc.vector.quantize_mx(
                    out=w3_codes[chunk][:].bitcast(FP8X4), scales=w3_scales[chunk][:],
                    in_=w3_bf[:].rearrange("p w t -> p (w t)"),
                )

        def features(c):
            h2_bank, h1_bank = banks[3 + 2 * ((c - 1) % 2):][:2]
            for a in range(2):
                cols = slice(a * P, (a + 1) * P)
                nc.tensor.matmul_mx(
                    out=h1_bank[:],
                    lhsT=w1_codes[c][:, cols].bitcast(FP8X4), lhsT_scale=w1_scales[c][:, cols],
                    rhs=v_picked[a][:].bitcast(FP8X4), rhs_scale=v_picked_scales[4 * a:P, :],
                    start=(a == 0), stop=(a == 1),
                )
            nc.scalar.activation(h2_sb[c % 2][:], h1_bank[:], ACT.Tanh)
            nc.scalar.activation(h1_sb[c % 2][:], h2_sb[c % 2][:], ACT.Copy, scale=g1_cols[:, c:c + 1])
            chunk, first = divmod(c * P, W_CHUNK)
            cols = slice(first, first + P)
            nc.tensor.matmul_mx(
                out=h2_bank[:],
                lhsT=w3_codes[chunk][:, cols].bitcast(FP8X4), lhsT_scale=w3_scales[chunk][:, cols],
                rhs=d_codes[:].bitcast(FP8X4), rhs_scale=d_scales[:],
                start=True, stop=True,
            )
            nc.scalar.copy(out=h2_sb[c % 2][:], in_=h2_bank[:])

        def place(c):
            nc.vector.tensor_tensor(pages_a[c % 2][:].indirect(list_pa[:]), h1_sb[c % 2][:], wg1_sb[:], ALU.mult)
            nc.vector.tensor_tensor(pages_b[c % 2][:].indirect(list_pb[:]), h2_sb[c % 2][:], wg2_sb[:], ALU.mult)

        def turn_sum(c):
            for half in range(2):
                bank = banks[(1 if c + 1 < SLICES else 5) + half]
                for n, source in enumerate((cat_sb[c], pages_a[c % 2])):
                    for j in range(4):
                        first = half * BANK + j * P
                        nc.tensor.matmul(
                            bank[:, j * P:(j + 1) * P], source[:, first:first + P], ident[:],
                            start=(n == 0 and j == 0), stop=(n == 1 and j == 3), is_transpose=True,
                        )
                nc.scalar.copy(
                    out=sum_turned[c % 2][half][:].rearrange("p (j u q e) -> p j u q e", j=4, u=2, e=2),
                    in_=bank[:].rearrange("p (j q u e) -> p j u q e", j=4, u=2, e=2),
                )

        def maximum(c):
            a, place_in_pass = divmod(c, 4)
            for half in range(2):
                bank = banks[3 + 2 * (c % 2) + half]
                for j in range(4):
                    first = half * BANK + j * P
                    nc.tensor.transpose(bank[:, j * P:(j + 1) * P], pages_b[c % 2][:, first:first + P], ident[:])
                nc.vector.tensor_tensor(
                    z_turned[a][half][:, :, :, place_in_pass * 64:(place_in_pass + 1) * 64],
                    bank[:].rearrange("p (j u x) -> p j u x", j=4, u=2),
                    sum_turned[c % 2][half][:].rearrange("p (j u x) -> p j u x", j=4, u=2),
                    ALU.max,
                )

        z_bf = {}

        def quantise_z(a, k):
            bank = banks[((0, 7, 0, 7), (3, 4, 5, 6))[a][k]]
            for j in range(2):
                for u in range(2):
                    first = (2 * j + u) * P
                    pairs = z_turned[a][k // 2][:, 2 * (k % 2) + j, u, :].bitcast(F32)
                    nc.tensor.transpose(bank[:, first:first + P], pairs, ident[:])
            group = 2 - a
            if k % group == 0:
                z_bf[a] = shared("stage", 12, "z_bf%d_%d" % (a, k), [P, group * PACK * Y_CHUNK], BF16)
            part = slice(k % group * PACK * Y_CHUNK, (k % group + 1) * PACK * Y_CHUNK)
            nc.scalar.copy(
                out=z_bf[a][:, part].bitcast(F32).rearrange("p (j s u) -> p j s u", j=2, u=2),
                in_=bank[:].rearrange("p (j u s) -> p j s u", j=2, u=2),
            )
            if (k + 1) % group == 0:
                cols = slice((k + 1 - group) * Y_CHUNK, (k + 1) * Y_CHUNK)
                nc.vector.quantize_mx(out=z_codes[a][:, cols].bitcast(FP8X4), scales=z_scales[a][:, cols], in_=z_bf[a][:])

        w4_dealt = {}
        w4_dealt_scales = held("w4_dealt_scales", [P, 2, PACK, P], U8)

        def deal_w4_words(a, tile):
            w4_dealt[a] = tile
            nc.vector.tensor_copy(
                out=tile[:].rearrange("p t (q b) -> p t q b", b=2),
                in_=w4_raw[:, a, :].rearrange("p (q t b) -> p t q b", t=PACK, b=2),
            )

        y_codes = held("y_codes", [P, T2], U32)
        y_scales = held("y_scales", [P, T2], U8)
        out_rows = out_0.rearrange("(p t) j -> p t j", t=PACK)
        out_words = words_of(out_1[0])
        y_banks = ((0, 7), (1, 2), (3, 4), (5, 6))

        def last_product(a, k):
            cols = slice(k * Y_CHUNK, (k + 1) * Y_CHUNK)
            for t in range(PACK):
                pair, i = divmod(t, 2)
                nc.tensor.matmul_mx(
                    out=banks[y_banks[k][pair]][:, i * Y_CHUNK:(i + 1) * Y_CHUNK],
                    lhsT=w4_dealt[a][:, t, :].bitcast(FP4X4), lhsT_scale=w4_dealt_scales[:, a, t, :],
                    rhs=z_codes[a][:, cols].bitcast(FP8X4), rhs_scale=z_scales[a][:, cols],
                    start=(a == 0 and i == 0), stop=(a == 1 and i == 1),
                )

        def finish(k):
            cols = slice(k * Y_CHUNK, (k + 1) * Y_CHUNK)
            y = shared("stage", 12, "y%d" % k, [P, PACK, Y_CHUNK], F32)
            last_product(1, k)
            for pair in range(2):
                nc.vector.tensor_tensor(
                    y[:, 2 * pair:2 * pair + 2, :], banks[y_banks[k][pair]][:].rearrange("p (i s) -> p i s", i=2),
                    res_sb[k // 2][:, 2 * pair:2 * pair + 2, (k % 2) * Y_CHUNK:(k % 2 + 1) * Y_CHUNK], ALU.add,
                )
                nc.sync.dma_start(out=out_rows[:, 2 * pair:2 * pair + 2, cols], in_=y[:, 2 * pair:2 * pair + 2, :])
            y_bf = shared("stage", 12, "y_bf%d" % k, [P, Y_CHUNK, PACK], BF16)
            if k + 1 < T2 // Y_CHUNK:
                round_and_interleave(y_bf[:], y[:])
            else:
                nc.vector.tensor_copy(
                    out=y_bf[:].rearrange("p (g i) t -> p g t i", i=4), in_=y[:].rearrange("p t (g i) -> p g t i", i=4)
                )
            nc.vector.quantize_mx(
                out=y_codes[:, cols].bitcast(FP8X4), scales=y_scales[:, cols], in_=y_bf[:].rearrange("p s t -> p (s t)")
            )

        quantise_weights(0)
        quantise_weights(1)
        deal_w4_words(0, held("w4_dealt0", [P, PACK, 2 * P], U8))
        nc.vector.tensor_copy(out=w4_dealt_scales[:], in_=w4_raw_scales[:].rearrange("p a (q t) -> p a t q", t=PACK))
        for c in range(SLICES):
            features(c)
            place(c)
            if c + 2 < SLICES:
                quantise_weights(c + 2)
            if c > 0:
                turn_sum(c - 1)
                maximum(c - 1)
            for k in {5: (0,), 6: (1,), 7: (2, 3)}.get(c, ()):
                quantise_z(0, k)
        last_product(0, 0)
        turn_sum(SLICES - 1)
        last_product(0, 1)
        maximum(SLICES - 1)
        deal_w4_words(1, shared("sum1_1", 1, "w4_dealt1", [P, PACK, 2 * P], U8))
        for k in range(T2 // Y_CHUNK):
            quantise_z(1, k)
        finish(0)
        finish(1)
        for k in (2, 3):
            last_product(0, k)
            finish(k)
        for cols in (slice(0, T2 - Y_CHUNK), slice(T2 - Y_CHUNK, T2)):
            nc.sync.dma_start(out=out_words[:, cols], in_=y_codes[:, cols].bitcast(I32))
        for q in range(4):
            queue = nc.sync if q % 2 == 0 else nc.scalar
            queue.dma_start(out=out_2[0, 4 * q:4 * q + 4, :].bitcast(I32), in_=y_scales[32 * q:32 * q + 4, :].bitcast(I32))
